import numpy as np
import ml_dtypes


def mxq(x, axis, fmt="e4m3"):
    dtype, down = {"e4m3": (ml_dtypes.float8_e4m3fn, 7), "e5m2": (ml_dtypes.float8_e5m2, 14)}[fmt]
    v = np.moveaxis(np.asarray(x, np.float32).astype(ml_dtypes.bfloat16).astype(np.float64), axis, -1)
    blocks = v.reshape(v.shape[:-1] + (-1, 32))
    amax = np.abs(blocks).max(-1, keepdims=True)
    byte = np.maximum(np.where(amax > 0, np.frexp(amax)[1] - 1 + 127, 0) - down, 1)
    scale = np.exp2(byte - 127.0)
    codes = (blocks / scale).astype(np.float32).astype(dtype).astype(np.float64)
    return np.moveaxis((codes * scale).reshape(v.shape), -1, axis)


WIDE = False


def mx_kscale(k):
    if not WIDE:
        return np.ones(k)
    levels = np.array([10, -10, 5, -5, 0])
    if k % 512:
        return np.exp2(np.random.permutation(np.resize(levels, k // 32))).repeat(32)
    a = np.empty((k // 512, 16))
    for p in range(k // 512):
        a[p, :8] = np.random.permutation(np.resize(levels, 8))
        for g in range(8):
            far = levels[np.abs(levels - a[p, g]) >= 10]
            a[p, g + 8] = far[np.random.randint(len(far))]
    return np.exp2(a.ravel()).repeat(32)


def f64(x):
    return np.asarray(x).astype(np.float64)


def striped(idx):
    return np.tile(idx.reshape(-1, 16).T, (8, 1)).astype(np.uint16)


def unstriped(offs):
    return offs[:16].T.reshape(-1).astype(np.int64)


def striped8(idx):
    return np.concatenate([x.reshape(-1, 16).T for x in idx]).astype(np.uint16)


def runs(offs, k):
    lists = np.stack([offs[16 * r : 16 * r + 16].T.reshape(-1) for r in range(8)]).astype(np.int64)
    return lists[np.arange(k) % 512 // 64]


def pack_weight(w):
    k, n = w.shape
    w = f64(np.asarray(w, np.float32).astype(ml_dtypes.bfloat16)).reshape(k // 32, 32, n)
    amax = np.abs(w).max(1)
    byte = np.clip(np.where(amax > 0, np.frexp(amax)[1] - 1 + 127 - 7, 1), 1, 254)
    scaled = (w * np.exp2(127.0 - byte)[:, None, :]).reshape(k, n).astype(np.float32)
    words = np.ascontiguousarray(scaled.reshape(k // 512, 128, 4, n).transpose(0, 1, 3, 2)).astype(ml_dtypes.float8_e4m3fn).view(np.uint8)
    return words, np.ascontiguousarray(byte.astype(np.uint8).reshape(k // 512, 16, n))


def unpack_weight(words, scales):
    g, p, n, _ = words.shape
    vals = np.ascontiguousarray(words).view(ml_dtypes.float8_e4m3fn).astype(np.float64) * np.repeat(np.exp2(scales.astype(np.float64) - 127.0), 8, axis=1)[..., None]
    return vals.transpose(0, 1, 3, 2).reshape(g * 512, n)


def relu(v):
    return np.maximum(v, 0.0)


def sigmoid(v):
    return 1.0 / (1.0 + np.exp(-np.maximum(v, -700.0)))


K, T, S, V, H = 512, 2048, 512, 512, 512


def setup_inputs():
    n = np.random.standard_normal
    s = mx_kscale(K)[:, None]
    u = mx_kscale(S)
    packed_xT = pack_weight(n((K, T)) * s)
    return {
        "x_words": packed_xT[0],
        "x_scales": packed_xT[1],
        "w1": (n((K, H)) / np.sqrt(K) / s).astype(np.float32),
        "w2": (n((K, H)) / np.sqrt(K) / s).astype(np.float32),
        "ga": (np.random.uniform(0.5, 1.5, (H, 1)) * u[:, None]).astype(np.float32),
        "gb": (np.random.uniform(0.5, 1.5, (H, 1)) / u[:, None]).astype(np.float32),
        "offs": striped(np.random.permutation(T)[:S]),
        "two": striped(np.random.permutation(T)[:V]),
        "n1": striped8(np.stack([np.random.permutation(S) for _ in range(8)])),
        "n2": striped8(np.stack([np.random.permutation(S) for _ in range(8)])),
        "n3": striped8(np.stack([np.random.permutation(V) for _ in range(8)])),
        "n4": striped8(np.stack([np.random.permutation(V) for _ in range(8)])),
        "n5": striped8(np.stack([np.random.permutation(V) for _ in range(8)])),
        "n6": striped8(np.stack([np.random.permutation(V) for _ in range(8)])),
        "n7": striped8(np.stack([np.random.permutation(V) for _ in range(8)])),
    }


def reference(x_words, x_scales, w1, w2, ga, gb, offs, two, n1, n2, n3, n4, n5, n6, n7):
    xq = unpack_weight(x_words, x_scales)[:, unstriped(offs)]
    a = mxq(f64(w1), 0, "e4m3").T @ xq
    pa = a - (a[np.arange(H)[:, None], runs(n1, H)])
    pb = a[np.arange(H)[:, None], runs(n2, H)] - a
    z = f64(ga) * (relu(np.minimum(pa, pb)) - (relu(-1.0 * np.maximum(pa, pb))))
    x_two = unpack_weight(x_words, x_scales)[:, unstriped(two)]
    b = mxq(f64(w2), 0, "e4m3").T @ x_two
    pa2 = b[np.arange(H)[:, None], runs(n3, H)]
    z2 = f64(gb) * (pa2 + (sigmoid(b[np.arange(H)[:, None], runs(n4, H)])) * (b[np.arange(H)[:, None], runs(n5, H)] - pa2))
    s = 0.0625 * ((mxq(z, 0, "e4m3").T @ mxq(z2, 0, "e4m3")))
    st = s * (sigmoid(s[np.arange(S)[:, None], runs(n6, S)]))
    return st - (st[np.arange(S)[:, None], runs(n7, S)])

@@ -1,0 +1,289 @@
+from contextlib import ExitStack
+
+import concourse.mybir as mybir
+
+K, T, S, V, H = 512, 2048, 512, 512, 512
+FLOPS = 3 * 2 * 512 * 512 * 512
+
+F32 = mybir.dt.float32
+BF16 = mybir.dt.bfloat16
+U32 = mybir.dt.uint32
+I32 = mybir.dt.int32
+U16 = mybir.dt.uint16
+U8 = mybir.dt.uint8
+FP8X4 = mybir.dt.float8_e4m3fn_x4
+ALU = mybir.AluOpType
+ACT = mybir.ActivationFunctionType
+
+P = 128
+PACK = 4
+HALF = 256
+CHUNKS = [(0, 256), (256, 256)]
+
+
+def tile_picked_kqminmodlerphopg_none_p_kernel(
+    tc, x_words, x_scales, w1, w2, ga, gb, offs, two, n1, n2, n3, n4, n5, n6, n7, out
+):
+    nc = tc.nc
+    with ExitStack() as ctx:
+        keep = ctx.enter_context(tc.tile_pool(name="keep", bufs=1))
+        psum = ctx.enter_context(tc.psum_pool(name="psum", bufs=1))
+
+        def sb(name, shape, dtype):
+            return keep.tile(shape, dtype, name=name, align_bytes=64)
+
+        def load_list(name, src):
+            tile = sb(name, [P, S // 16], U16)
+            nc.sync.dma_start(tile[:], src)
+            return tile
+
+        def entries(lst, lo, n):
+            return lst[:, lo // 16 : (lo + n) // 16]
+
+        x_sc = sb("x_sc", [P, T], U8)
+        nc.gpsimd.memset(x_sc[:].bitcast(I32), 0)
+        l_two = load_list("l_two", two)
+        x_w = sb("x_w", [P, T], U32)
+        nc.sync.dma_start(x_w[:].bitcast(I32), x_words[0].rearrange("p n t -> p (n t)").bitcast(I32))
+        for q in range(4):
+            nc.gpsimd.dma_start(x_sc[32 * q : 32 * q + 4, :].bitcast(I32), x_scales[0, 4 * q : 4 * q + 4, :].bitcast(I32))
+
+        def load_weight(name, w):
+            halves = []
+            for h in range(2):
+                raw = sb(f"{name}_raw{h}", [P, PACK, HALF], F32)
+                nc.sync.dma_start(raw[:], w[:, h * HALF : (h + 1) * HALF].rearrange("(p j) c -> p j c", j=PACK))
+                halves.append(raw)
+            return halves
+
+        def load_gain(name, g):
+            tile = sb(name, [P, PACK], F32)
+            nc.gpsimd.dma_start(tile[:], g.rearrange("(p t) o -> p (t o)", t=PACK))
+            return tile
+
+        l_offs = load_list("l_offs", offs)
+        w2_raw = load_weight("w2", w2)
+        gb_sb = load_gain("gb_sb", gb)
+        l_n3 = load_list("l_n3", n3)
+        l_n5 = load_list("l_n5", n5)
+        l_n4 = load_list("l_n4", n4)
+        w1_raw = load_weight("w1", w1)
+        ga_sb = load_gain("ga_sb", ga)
+        l_n1 = load_list("l_n1", n1)
+        l_n2 = load_list("l_n2", n2)
+        l_n6 = load_list("l_n6", n6)
+        l_n7 = load_list("l_n7", n7)
+
+        def deal(copy, grouped, m0, planes):
+            count = planes.shape[2] // PACK
+            copy(
+                grouped[:, :, m0 : m0 + count, :].rearrange("p (u i) m j -> p u m j i", i=2),
+                planes.rearrange("p j (m u i) -> p u m j i", u=2, i=2),
+            )
+
+        def pick(name, lst):
+            words = sb(f"{name}_w", [P, S], U32)
+            scales = sb(f"{name}_s", [P, S], U8)
+            nc.vector.tensor_copy(words[:], x_w[:].indirect(lst[:]))
+            nc.vector.tensor_copy(scales[:], x_sc[:].indirect(lst[:]))
+            return words, scales
+
+        def quantize(name, grouped_flat):
+            width = grouped_flat.shape[1] // PACK
+            words = sb(f"{name}_w", [P, width], U32)
+            scales = sb(f"{name}_s", [P, width], U8)
+            nc.vector.quantize_mx(out=words[:].bitcast(FP8X4), scales=scales[:], in_=grouped_flat)
+            return words, scales
+
+        def mx(acc, lhs, lhs_cols, rhs):
+            nc.tensor.matmul_mx(
+                out=acc,
+                lhsT=lhs[0][:, lhs_cols].bitcast(FP8X4),
+                lhsT_scale=lhs[1][:, lhs_cols],
+                rhs=rhs[0][:].bitcast(FP8X4),
+                rhs_scale=rhs[1][:],
+                start=True,
+                stop=True,
+            )
+
+        def cast_weight(name, raw, copies):
+            grouped = sb(f"{name}_grp", [P, PACK, P, PACK], BF16)
+            for h in range(2):
+                deal(copies[h], grouped, h * HALF // PACK, raw[h][:])
+            return grouped
+
+        def project(name, grouped, picked, bank0):
+            accs = []
+            for t in range(PACK):
+                wq = quantize(f"{name}_q{t}", grouped[:, t, :, :].rearrange("p m j -> p (m j)"))
+                acc = psum.tile([P, S], F32, name=f"{name}_acc{t}", tag=f"bank{bank0 + t}")
+                mx(acc[:], wq, slice(0, P), picked)
+                accs.append(acc)
+            return accs
+
+        def fetch(on_vector, dst, window, lst, lo, n):
+            if on_vector:
+                nc.vector.tensor_copy(dst, window[:].indirect(entries(lst, lo, n)))
+            else:
+                nc.scalar.activation(dst, window[:].indirect(entries(lst, lo, n)), ACT.Copy)
+
+        def scaled(on_vector, dst, acc, gain):
+            if on_vector:
+                nc.vector.tensor_scalar(dst, acc, gain, None, ALU.mult)
+            else:
+                nc.scalar.activation(dst, acc, ACT.Copy, scale=gain)
+
+        z_planes = sb("z_planes", [P, PACK, S], F32)
+        cols = [slice(h * HALF, (h + 1) * HALF) for h in range(2)]
+        a_val = [sb(f"a{t}", [P, S], F32) for t in range(PACK)]
+        g1 = [sb(f"g1_{t}", [P, S], F32) for t in range(PACK)]
+        g2 = [sb(f"g2_{t}", [P, S], F32) for t in range(PACK)]
+
+        def fetch_a(t, v_evac=False, v_fetch=()):
+            scaled(v_evac, a_val[t][:], a_ps[t][:], ga_sb[:, t : t + 1])
+            for h in range(2):
+                fetch((1, h) in v_fetch, g1[t][:, cols[h]], a_val[t], l_n1, h * HALF, HALF)
+                fetch((2, h) in v_fetch, g2[t][:, cols[h]], a_val[t], l_n2, h * HALF, HALF)
+
+        def limit_a(t):
+            pa = sb(f"pa_{t}", [P, S], F32)
+            pb = sb(f"pb_{t}", [P, S], F32)
+            low = sb(f"low_{t}", [P, S], F32)
+            for c in cols:
+                nc.vector.tensor_tensor(pa[:, c], a_val[t][:, c], g1[t][:, c], ALU.subtract)
+                nc.vector.tensor_tensor(pb[:, c], g2[t][:, c], a_val[t][:, c], ALU.subtract)
+            for c in cols:
+                nc.vector.scalar_tensor_tensor(low[:, c], pb[:, c], 0.0, pa[:, c], ALU.min, ALU.max)
+            for c in cols:
+                nc.vector.scalar_tensor_tensor(z_planes[:, t, c], pb[:, c], 0.0, low[:, c], ALU.max, ALU.min)
+
+        CH = CHUNKS
+        b_gain = [sb(f"b_gain{t}", [P, V], F32) for t in range(PACK)]
+        b_sig = [sb(f"b_sig{t}", [P, V], F32) for t in range(PACK)]
+        near = [sb(f"near{h}", [P, PACK, n], F32) for h, (lo, n) in enumerate(CH)]
+        step = [sb(f"step{h}", [P, PACK, n], F32) for h, (lo, n) in enumerate(CH)]
+        move = [sb(f"move{h}", [P, PACK, n], F32) for h, (lo, n) in enumerate(CH)]
+        gate_b = [sb(f"gate_b{h}", [P, PACK, n], F32) for h, (lo, n) in enumerate(CH)]
+
+        def open_b(t, v_evac=False):
+            scaled(v_evac, b_gain[t][:], b_ps[t][:], gb_sb[:, t : t + 1])
+            nc.scalar.activation(b_sig[t][:], b_ps[t][:], ACT.Sigmoid)
+
+        def near_b(ts, h, on_vector=False):
+            lo, n = CH[h]
+            for t in ts:
+                fetch(on_vector, near[h][:, t, :], b_gain[t], l_n3, lo, n)
+
+        def blend_b(ts, h, unfused=False):
+            lo, n = CH[h]
+            if unfused:
+                for t in ts:
+                    fetch(False, gate_b[h][:, t, :], b_sig[t], l_n4, lo, n)
+            for t in ts:
+                nc.vector.tensor_tensor(
+                    step[h][:, t, :], b_gain[t][:].indirect(entries(l_n5, lo, n)), near[h][:, t, :], ALU.subtract
+                )
+            for t in ts:
+                if unfused:
+                    nc.vector.tensor_tensor(move[h][:, t, :], gate_b[h][:, t, :], step[h][:, t, :], ALU.mult)
+                else:
+                    nc.vector.tensor_tensor(
+                        move[h][:, t, :], b_sig[t][:].indirect(entries(l_n4, lo, n)), step[h][:, t, :], ALU.mult
+                    )
+
+        def close_b(h):
+            grouped = sb(f"z2_grp{h}", [P, CH[h][1], PACK], BF16)
+            nc.vector.tensor_tensor(
+                grouped[:].rearrange("p (c i) t -> p c t i", i=2),
+                near[h][:].rearrange("p t (c i) -> p c t i", i=2),
+                move[h][:].rearrange("p t (c i) -> p c t i", i=2),
+                ALU.add,
+            )
+            return quantize(f"z2_q{h}", grouped[:].rearrange("p c t -> p (c t)"))
+
+        s_val = [sb(f"s_val{t}", [P, V], F32) for t in range(PACK)]
+        s_sig = [sb(f"s_sig{t}", [P, V], F32) for t in range(PACK)]
+
+        def scores(zq, z2q, h):
+            lo, n = CH[h]
+            accs = []
+            for t in range(PACK):
+                acc = psum.tile([P, n], F32, name=f"s_acc{h}_{t}", tag=f"bank{PACK * (h % 2) + t}")
+                mx(acc[:], zq, slice(t * P, (t + 1) * P), z2q)
+                accs.append(acc)
+            return accs
+
+        def open_s(accs, h, t):
+            lo, n = CH[h]
+            nc.scalar.activation(s_sig[t][:, lo : lo + n], accs[t][:], ACT.Sigmoid, scale=0.0625)
+            nc.scalar.activation(s_val[t][:, lo : lo + n], accs[t][:], ACT.Copy, scale=0.0625)
+
+        out_rows = out.rearrange("(m t) v -> t m v", t=PACK)
+        st = [sb(f"st{t}", [P, V], F32) for t in range(PACK)]
+        hop = [sb(f"hop{t}", [P, V], F32) for t in range(PACK)]
+        res = [sb(f"res{t}", [P, V], F32) for t in range(PACK)]
+
+        def gate(t):
+            for h in range(2):
+                nc.vector.tensor_tensor(
+                    st[t][:, cols[h]], s_sig[t][:].indirect(entries(l_n6, h * HALF, HALF)), s_val[t][:, cols[h]], ALU.mult
+                )
+
+        def hop_s(t, v_fetch=()):
+            for h in range(2):
+                fetch(h in v_fetch, hop[t][:, cols[h]], st[t], l_n7, h * HALF, HALF)
+
+        def finish(t):
+            for h in range(2):
+                nc.vector.tensor_tensor(res[t][:, cols[h]], st[t][:, cols[h]], hop[t][:, cols[h]], ALU.subtract)
+                nc.sync.dma_start(out_rows[t][:, cols[h]], res[t][:, cols[h]])
+
+        z_grp = sb("z_grp", [P, PACK, P, PACK], BF16)
+        xb = pick("xb", l_two)
+        w2_grp = cast_weight("w2", w2_raw, [nc.scalar.copy, nc.scalar.copy])
+        b_ps = project("w2", w2_grp, xb, 0)
+        xa = pick("xa", l_offs)
+        w1_grp = cast_weight("w1", w1_raw, [nc.scalar.copy, nc.scalar.copy])
+        open_b(0, True)
+        near_b([0], 0, True)
+        open_b(1, True)
+        near_b([1], 0, True)
+        a_ps = project("w1", w1_grp, xa, PACK)
+        blend_b([0, 1], 0)
+        fetch_a(0)
+        fetch_a(1)
+        limit_a(0)
+        open_b(2)
+        open_b(3)
+        near_b([2, 3], 0)
+        limit_a(1)
+        fetch_a(2)
+        blend_b([2, 3], 0)
+        fetch_a(3)
+        limit_a(2)
+        z2q0 = close_b(0)
+        limit_a(3)
+        deal(nc.vector.tensor_copy, z_grp, 0, z_planes[:])
+        zq = quantize("z_q", z_grp[:].rearrange("p t m j -> p (t m j)"))
+        near_b([0, 1, 2, 3], 1)
+        s0 = scores(zq, z2q0, 0)
+        blend_b([0, 1], 1, True)
+        blend_b([2, 3], 1, True)
+        for t in range(PACK):
+            open_s(s0, 0, t)
+        z2q1 = close_b(1)
+        s1 = scores(zq, z2q1, 1)
+        for t in range(PACK):
+            open_s(s1, 1, t)
+        gate(0)
+        gate(1)
+        hop_s(0)
+        finish(0)
+        gate(2)
+        hop_s(1)
+        finish(1)
+        gate(3)
+        hop_s(2)
+        finish(2)
+        hop_s(3)
+        finish(3)

@@ -40,34 +40,30 @@ def tile_picked_kqminmodlerphopg_none_p_kernel(
         def entries(lst, lo, n):
             return lst[:, lo // 16 : (lo + n) // 16]
 
-        x_sc = sb("x_sc", [P, T], U8)
-        nc.gpsimd.memset(x_sc[:].bitcast(I32), 0)
-        l_two = load_list("l_two", two)
-        x_w = sb("x_w", [P, T], U32)
-        nc.sync.dma_start(x_w[:].bitcast(I32), x_words[0].rearrange("p n t -> p (n t)").bitcast(I32))
-        for q in range(4):
-            nc.gpsimd.dma_start(x_sc[32 * q : 32 * q + 4, :].bitcast(I32), x_scales[0, 4 * q : 4 * q + 4, :].bitcast(I32))
-
         def load_weight(name, w):
-            halves = []
-            for h in range(2):
-                raw = sb(f"{name}_raw{h}", [P, PACK, HALF], F32)
-                nc.sync.dma_start(raw[:], w[:, h * HALF : (h + 1) * HALF].rearrange("(p j) c -> p j c", j=PACK))
-                halves.append(raw)
-            return halves
+            raw = sb(f"{name}_raw", [P, PACK, H], F32)
+            nc.sync.dma_start(raw[:], w.rearrange("(p j) c -> p j c", j=PACK))
+            return raw
 
         def load_gain(name, g):
             tile = sb(name, [P, PACK], F32)
-            nc.gpsimd.dma_start(tile[:], g.rearrange("(p t) o -> p (t o)", t=PACK))
+            nc.sync.dma_start(tile[:], g.rearrange("(p t) o -> p (t o)", t=PACK))
             return tile
 
-        l_offs = load_list("l_offs", offs)
+        x_sc = sb("x_sc", [P, T], U8)
+        nc.vector.memset(x_sc[:].bitcast(I32), 0)
+        l_two = load_list("l_two", two)
         w2_raw = load_weight("w2", w2)
+        for q in range(4):
+            nc.sync.dma_start(x_sc[32 * q : 32 * q + 4, :].bitcast(I32), x_scales[0, 4 * q : 4 * q + 4, :].bitcast(I32))
+        l_offs = load_list("l_offs", offs)
+        x_w = sb("x_w", [P, T], U32)
+        nc.sync.dma_start(x_w[:].bitcast(I32), x_words[0].rearrange("p n t -> p (n t)").bitcast(I32))
+        w1_raw = load_weight("w1", w1)
         gb_sb = load_gain("gb_sb", gb)
         l_n3 = load_list("l_n3", n3)
         l_n5 = load_list("l_n5", n5)
         l_n4 = load_list("l_n4", n4)
-        w1_raw = load_weight("w1", w1)
         ga_sb = load_gain("ga_sb", ga)
         l_n1 = load_list("l_n1", n1)
         l_n2 = load_list("l_n2", n2)
@@ -81,12 +77,15 @@ def tile_picked_kqminmodlerphopg_none_p_kernel(
                 planes.rearrange("p j (m u i) -> p u m j i", u=2, i=2),
             )
 
-        def pick(name, lst):
-            words = sb(f"{name}_w", [P, S], U32)
+        def pick_scales(name, lst):
             scales = sb(f"{name}_s", [P, S], U8)
-            nc.vector.tensor_copy(words[:], x_w[:].indirect(lst[:]))
             nc.vector.tensor_copy(scales[:], x_sc[:].indirect(lst[:]))
-            return words, scales
+            return scales
+
+        def pick_words(name, lst):
+            words = sb(f"{name}_w", [P, S], U32)
+            nc.vector.tensor_copy(words[:], x_w[:].indirect(lst[:]))
+            return words
 
         def quantize(name, grouped_flat):
             width = grouped_flat.shape[1] // PACK
@@ -106,18 +105,22 @@ def tile_picked_kqminmodlerphopg_none_p_kernel(
                 stop=True,
             )
 
-        def cast_weight(name, raw, copies):
+        def cast_weight(name, raw, vector_cols):
             grouped = sb(f"{name}_grp", [P, PACK, P, PACK], BF16)
-            for h in range(2):
-                deal(copies[h], grouped, h * HALF // PACK, raw[h][:])
+            if vector_cols:
+                deal(nc.vector.tensor_copy, grouped, 0, raw[:, :, :vector_cols])
+            if vector_cols < H:
+                deal(nc.scalar.copy, grouped, vector_cols // PACK, raw[:, :, vector_cols:])
             return grouped
 
-        def project(name, grouped, picked, bank0):
+        def quantize_weight(name, grouped):
+            return [quantize(f"{name}_q{t}", grouped[:, t, :, :].rearrange("p m j -> p (m j)")) for t in range(PACK)]
+
+        def project(name, wq, picked, bank0):
             accs = []
             for t in range(PACK):
-                wq = quantize(f"{name}_q{t}", grouped[:, t, :, :].rearrange("p m j -> p (m j)"))
                 acc = psum.tile([P, S], F32, name=f"{name}_acc{t}", tag=f"bank{bank0 + t}")
-                mx(acc[:], wq, slice(0, P), picked)
+                mx(acc[:], wq[t], slice(0, P), picked)
                 accs.append(acc)
             return accs
 
@@ -163,10 +166,13 @@ def tile_picked_kqminmodlerphopg_none_p_kernel(
         near = [sb(f"near{h}", [P, PACK, n], F32) for h, (lo, n) in enumerate(CH)]
         step = [sb(f"step{h}", [P, PACK, n], F32) for h, (lo, n) in enumerate(CH)]
         move = [sb(f"move{h}", [P, PACK, n], F32) for h, (lo, n) in enumerate(CH)]
+        far = [sb(f"far{h}", [P, PACK, n], F32) for h, (lo, n) in enumerate(CH)]
         gate_b = [sb(f"gate_b{h}", [P, PACK, n], F32) for h, (lo, n) in enumerate(CH)]
 
-        def open_b(t, v_evac=False):
-            scaled(v_evac, b_gain[t][:], b_ps[t][:], gb_sb[:, t : t + 1])
+        def open_gain(t):
+            nc.scalar.activation(b_gain[t][:], b_ps[t][:], ACT.Copy, scale=gb_sb[:, t : t + 1])
+
+        def open_sig(t):
             nc.scalar.activation(b_sig[t][:], b_ps[t][:], ACT.Sigmoid)
 
         def near_b(ts, h, on_vector=False):
@@ -174,49 +180,58 @@ def tile_picked_kqminmodlerphopg_none_p_kernel(
             for t in ts:
                 fetch(on_vector, near[h][:, t, :], b_gain[t], l_n3, lo, n)
 
-        def blend_b(ts, h, unfused=False):
+        def fetch_b(dst, window, lst, ts, h):
             lo, n = CH[h]
-            if unfused:
-                for t in ts:
-                    fetch(False, gate_b[h][:, t, :], b_sig[t], l_n4, lo, n)
             for t in ts:
-                nc.vector.tensor_tensor(
-                    step[h][:, t, :], b_gain[t][:].indirect(entries(l_n5, lo, n)), near[h][:, t, :], ALU.subtract
-                )
-            for t in ts:
-                if unfused:
-                    nc.vector.tensor_tensor(move[h][:, t, :], gate_b[h][:, t, :], step[h][:, t, :], ALU.mult)
-                else:
-                    nc.vector.tensor_tensor(
-                        move[h][:, t, :], b_sig[t][:].indirect(entries(l_n4, lo, n)), step[h][:, t, :], ALU.mult
-                    )
+                fetch(False, dst[h][:, t, :], window[t], lst, lo, n)
 
-        def close_b(h):
-            grouped = sb(f"z2_grp{h}", [P, CH[h][1], PACK], BF16)
+        def step_b(ts, h, fused=True):
+            lo, n = CH[h]
+            for t in ts:
+                far_t = b_gain[t][:].indirect(entries(l_n5, lo, n)) if fused else far[h][:, t, :]
+                nc.vector.tensor_tensor(step[h][:, t, :], far_t, near[h][:, t, :], ALU.subtract)
+
+        def move_b(ts, h, fused=True):
+            lo, n = CH[h]
+            for t in ts:
+                gate_t = b_sig[t][:].indirect(entries(l_n4, lo, n)) if fused else gate_b[h][:, t, :]
+                nc.vector.tensor_tensor(move[h][:, t, :], gate_t, step[h][:, t, :], ALU.mult)
+
+        def close_b(h, lo=0, n=HALF):
+            grouped = sb(f"z2_grp{h}_{lo}", [P, n, PACK], BF16)
             nc.vector.tensor_tensor(
                 grouped[:].rearrange("p (c i) t -> p c t i", i=2),
-                near[h][:].rearrange("p t (c i) -> p c t i", i=2),
-                move[h][:].rearrange("p t (c i) -> p c t i", i=2),
+                near[h][:, :, lo : lo + n].rearrange("p t (c i) -> p c t i", i=2),
+                move[h][:, :, lo : lo + n].rearrange("p t (c i) -> p c t i", i=2),
                 ALU.add,
             )
-            return quantize(f"z2_q{h}", grouped[:].rearrange("p c t -> p (c t)"))
+            return grouped
+
+        def quant_b(h, lo, grouped):
+            return quantize(f"z2_q{h}_{lo}", grouped[:].rearrange("p c t -> p (c t)"))
 
         s_val = [sb(f"s_val{t}", [P, V], F32) for t in range(PACK)]
         s_sig = [sb(f"s_sig{t}", [P, V], F32) for t in range(PACK)]
 
-        def scores(zq, z2q, h):
-            lo, n = CH[h]
+        def scores(zq, z2q, lo, n, bank0):
             accs = []
             for t in range(PACK):
-                acc = psum.tile([P, n], F32, name=f"s_acc{h}_{t}", tag=f"bank{PACK * (h % 2) + t}")
+                acc = psum.tile([P, n], F32, name=f"s_acc{lo}_{t}", tag=f"bank{bank0 + t}")
                 mx(acc[:], zq, slice(t * P, (t + 1) * P), z2q)
                 accs.append(acc)
-            return accs
+            return accs, lo, n
 
-        def open_s(accs, h, t):
-            lo, n = CH[h]
+        def open_sig_s(sc, t):
+            accs, lo, n = sc
             nc.scalar.activation(s_sig[t][:, lo : lo + n], accs[t][:], ACT.Sigmoid, scale=0.0625)
-            nc.scalar.activation(s_val[t][:, lo : lo + n], accs[t][:], ACT.Copy, scale=0.0625)
+
+        def open_val_s(sc, t, on_vector=False):
+            accs, lo, n = sc
+            scaled(on_vector, s_val[t][:, lo : lo + n], accs[t][:], 0.0625)
+
+        def open_s(sc, t):
+            open_sig_s(sc, t)
+            open_val_s(sc, t)
 
         out_rows = out.rearrange("(m t) v -> t m v", t=PACK)
         st = [sb(f"st{t}", [P, V], F32) for t in range(PACK)]
@@ -229,61 +244,87 @@ def tile_picked_kqminmodlerphopg_none_p_kernel(
                     st[t][:, cols[h]], s_sig[t][:].indirect(entries(l_n6, h * HALF, HALF)), s_val[t][:, cols[h]], ALU.mult
                 )
 
-        def hop_s(t, v_fetch=()):
+        def gate_through(t):
             for h in range(2):
-                fetch(h in v_fetch, hop[t][:, cols[h]], st[t], l_n7, h * HALF, HALF)
+                nc.scalar.activation(s_sig[t][:, cols[h]], s_val[t][:].indirect(entries(l_n6, h * HALF, HALF)), ACT.Sigmoid)
+            for h in range(2):
+                nc.vector.tensor_tensor(st[t][:, cols[h]], s_sig[t][:, cols[h]], s_val[t][:, cols[h]], ALU.mult)
 
-        def finish(t):
-            for h in range(2):
-                nc.vector.tensor_tensor(res[t][:, cols[h]], st[t][:, cols[h]], hop[t][:, cols[h]], ALU.subtract)
-                nc.sync.dma_start(out_rows[t][:, cols[h]], res[t][:, cols[h]])
+        def hop_s(t, pieces=((0, HALF), (HALF, HALF)), v_fetch=()):
+            for lo, n in pieces:
+                fetch(lo in v_fetch, hop[t][:, lo : lo + n], st[t], l_n7, lo, n)
+
+        def finish(t, pieces=((0, V),)):
+            for lo, n in pieces:
+                c = slice(lo, lo + n)
+                nc.vector.tensor_tensor(res[t][:, c], st[t][:, c], hop[t][:, c], ALU.subtract)
+                nc.sync.dma_start(out_rows[t][:, c], res[t][:, c])
 
         z_grp = sb("z_grp", [P, PACK, P, PACK], BF16)
-        xb = pick("xb", l_two)
-        w2_grp = cast_weight("w2", w2_raw, [nc.scalar.copy, nc.scalar.copy])
-        b_ps = project("w2", w2_grp, xb, 0)
-        xa = pick("xa", l_offs)
-        w1_grp = cast_weight("w1", w1_raw, [nc.scalar.copy, nc.scalar.copy])
-        open_b(0, True)
-        near_b([0], 0, True)
-        open_b(1, True)
-        near_b([1], 0, True)
-        a_ps = project("w1", w1_grp, xa, PACK)
-        blend_b([0, 1], 0)
+        w2_grp = cast_weight("w2", w2_raw, 0)
+        xb_s = pick_scales("xb", l_two)
+        xa_s = pick_scales("xa", l_offs)
+        xb = (pick_words("xb", l_two), xb_s)
+        w2_q = quantize_weight("w2", w2_grp)
+        b_ps = project("w2", w2_q, xb, 0)
+        xa = (pick_words("xa", l_offs), xa_s)
+        w1_grp = cast_weight("w1", w1_raw, H)
+        w1_q = quantize_weight("w1", w1_grp)
+        a_ps = project("w1", w1_q, xa, PACK)
+        open_sig(0)
+        open_gain(0)
+        near_b([0], 0)
+        open_gain(1)
+        near_b([1], 0)
+        open_sig(1)
+        step_b([0, 1], 0)
+        move_b([0, 1], 0)
+        open_gain(2)
+        near_b([2], 0)
+        open_gain(3)
+        near_b([3], 0)
+        open_sig(2)
+        open_sig(3)
         fetch_a(0)
+        step_b([2, 3], 0)
+        move_b([2, 3], 0)
         fetch_a(1)
+        z2q0 = quant_b(0, 0, close_b(0))
         limit_a(0)
-        open_b(2)
-        open_b(3)
-        near_b([2, 3], 0)
-        limit_a(1)
         fetch_a(2)
-        blend_b([2, 3], 0)
+        limit_a(1)
+        near_b([0, 1], 1, True)
         fetch_a(3)
         limit_a(2)
-        z2q0 = close_b(0)
         limit_a(3)
+
+        fetch_b(gate_b, b_sig, l_n4, [0, 1], 1)
+        near_b([2, 3], 1)
+        fetch_b(far, b_gain, l_n5, [2, 3], 1)
+        fetch_b(gate_b, b_sig, l_n4, [2, 3], 1)
         deal(nc.vector.tensor_copy, z_grp, 0, z_planes[:])
         zq = quantize("z_q", z_grp[:].rearrange("p t m j -> p (t m j)"))
-        near_b([0, 1, 2, 3], 1)
-        s0 = scores(zq, z2q0, 0)
-        blend_b([0, 1], 1, True)
-        blend_b([2, 3], 1, True)
+        s0 = scores(zq, z2q0, 0, HALF, 0)
+        step_b([0, 1], 1, True)
+        move_b([0, 1], 1, False)
+        step_b([2, 3], 1, False)
+        move_b([2, 3], 1, False)
         for t in range(PACK):
-            open_s(s0, 0, t)
-        z2q1 = close_b(1)
-        s1 = scores(zq, z2q1, 1)
-        for t in range(PACK):
-            open_s(s1, 1, t)
+            open_s(s0, t)
+        s1 = scores(zq, quant_b(1, 0, close_b(1)), HALF, HALF, PACK)
+        open_s(s1, 0)
+        open_s(s1, 1)
         gate(0)
-        gate(1)
+        open_s(s1, 2)
         hop_s(0)
+        gate(1)
+        open_s(s1, 3)
         finish(0)
-        gate(2)
         hop_s(1)
+        gate(2)
         finish(1)
-        gate(3)
         hop_s(2)
+        gate(3)
         finish(2)
-        hop_s(3)
-        finish(3)
+        hop_s(3, ((0, HALF), (HALF, P), (HALF + P, P)))
+        finish(3, ((0, HALF), (HALF, P), (HALF + P, P)))

@@ -29,8 +29,8 @@ def tile_picked_kqminmodlerphopg_none_p_kernel(
         keep = ctx.enter_context(tc.tile_pool(name="keep", bufs=1))
         psum = ctx.enter_context(tc.psum_pool(name="psum", bufs=1))
 
-        def sb(name, shape, dtype):
-            return keep.tile(shape, dtype, name=name, align_bytes=64)
+        def sb(name, shape, dtype, tag=None):
+            return keep.tile(shape, dtype, name=name, tag=tag or name, align_bytes=64)
 
         def load_list(name, src):
             tile = sb(name, [P, S // 16], U16)
@@ -56,11 +56,11 @@ def tile_picked_kqminmodlerphopg_none_p_kernel(
         w2_raw = load_weight("w2", w2)
         for q in range(4):
             nc.sync.dma_start(x_sc[32 * q : 32 * q + 4, :].bitcast(I32), x_scales[0, 4 * q : 4 * q + 4, :].bitcast(I32))
-        l_offs = load_list("l_offs", offs)
+        gb_sb = load_gain("gb_sb", gb)
         x_w = sb("x_w", [P, T], U32)
         nc.sync.dma_start(x_w[:].bitcast(I32), x_words[0].rearrange("p n t -> p (n t)").bitcast(I32))
+        l_offs = load_list("l_offs", offs)
         w1_raw = load_weight("w1", w1)
-        gb_sb = load_gain("gb_sb", gb)
         l_n3 = load_list("l_n3", n3)
         l_n5 = load_list("l_n5", n5)
         l_n4 = load_list("l_n4", n4)
@@ -82,9 +82,10 @@ def tile_picked_kqminmodlerphopg_none_p_kernel(
             nc.vector.tensor_copy(scales[:], x_sc[:].indirect(lst[:]))
             return scales
 
-        def pick_words(name, lst):
+        def pick_words(name, lst, pieces=((0, S),)):
             words = sb(f"{name}_w", [P, S], U32)
-            nc.vector.tensor_copy(words[:], x_w[:].indirect(lst[:]))
+            for lo, n in pieces:
+                nc.vector.tensor_copy(words[:, lo : lo + n], x_w[:].indirect(entries(lst, lo, n)))
             return words
 
         def quantize(name, grouped_flat):
@@ -94,13 +95,13 @@ def tile_picked_kqminmodlerphopg_none_p_kernel(
             nc.vector.quantize_mx(out=words[:].bitcast(FP8X4), scales=scales[:], in_=grouped_flat)
             return words, scales
 
-        def mx(acc, lhs, lhs_cols, rhs):
+        def mx(acc, lhs, lhs_cols, rhs, rhs_cols=slice(None)):
             nc.tensor.matmul_mx(
                 out=acc,
                 lhsT=lhs[0][:, lhs_cols].bitcast(FP8X4),
                 lhsT_scale=lhs[1][:, lhs_cols],
-                rhs=rhs[0][:].bitcast(FP8X4),
-                rhs_scale=rhs[1][:],
+                rhs=rhs[0][:, rhs_cols].bitcast(FP8X4),
+                rhs_scale=rhs[1][:, rhs_cols],
                 start=True,
                 stop=True,
             )
@@ -116,12 +117,21 @@ def tile_picked_kqminmodlerphopg_none_p_kernel(
         def quantize_weight(name, grouped):
             return [quantize(f"{name}_q{t}", grouped[:, t, :, :].rearrange("p m j -> p (m j)")) for t in range(PACK)]
 
-        def project(name, wq, picked, bank0):
+        def project(name, wq, picked, bank0, spare_bank=None):
             accs = []
             for t in range(PACK):
-                acc = psum.tile([P, S], F32, name=f"{name}_acc{t}", tag=f"bank{bank0 + t}")
-                mx(acc[:], wq[t], slice(0, P), picked)
-                accs.append(acc)
+                if t == 0 and spare_bank is not None:
+                    parts = []
+                    for h, bank in enumerate((bank0, spare_bank)):
+                        acc = psum.tile([P, HALF], F32, name=f"{name}_acc{t}_{h}", tag=f"bank{bank}")
+                        c = slice(h * HALF, (h + 1) * HALF)
+                        mx(acc[:], wq[t], slice(0, P), picked, c)
+                        parts.append((acc, c))
+                else:
+                    acc = psum.tile([P, S], F32, name=f"{name}_acc{t}", tag=f"bank{bank0 + t}")
+                    mx(acc[:], wq[t], slice(0, P), picked)
+                    parts = [(acc, slice(0, S))]
+                accs.append(parts)
             return accs
 
         def fetch(on_vector, dst, window, lst, lo, n):
@@ -136,29 +146,49 @@ def tile_picked_kqminmodlerphopg_none_p_kernel(
             else:
                 nc.scalar.activation(dst, acc, ACT.Copy, scale=gain)
 
+        WIDE = 2 * S
         z_planes = sb("z_planes", [P, PACK, S], F32)
         cols = [slice(h * HALF, (h + 1) * HALF) for h in range(2)]
-        a_val = [sb(f"a{t}", [P, S], F32) for t in range(PACK)]
+        a_val = [sb(f"a{t}", [P, WIDE], F32) for t in range(PACK)]
         g1 = [sb(f"g1_{t}", [P, S], F32) for t in range(PACK)]
         g2 = [sb(f"g2_{t}", [P, S], F32) for t in range(PACK)]
 
-        def fetch_a(t, v_evac=False, v_fetch=()):
-            scaled(v_evac, a_val[t][:], a_ps[t][:], ga_sb[:, t : t + 1])
-            for h in range(2):
-                fetch((1, h) in v_fetch, g1[t][:, cols[h]], a_val[t], l_n1, h * HALF, HALF)
-                fetch((2, h) in v_fetch, g2[t][:, cols[h]], a_val[t], l_n2, h * HALF, HALF)
+        def fetch_a(t):
+            for acc, c in a_ps[t]:
+                scaled(False, a_val[t][:, c], acc[:], ga_sb[:, t : t + 1])
+            fetch(False, g1[t][:], a_val[t], l_n1, 0, S)
+            fetch(False, g2[t][:], a_val[t], l_n2, 0, S)
+
+        pa = [sb(f"pa_{t}", [P, S], F32) for t in range(PACK)]
+        pb = [sb(f"pb_{t}", [P, S], F32) for t in range(PACK)]
+        low = [sb(f"low_{t}", [P, S], F32) for t in range(PACK)]
+
+        def diff1(t, c=slice(0, S)):
+            nc.vector.tensor_tensor(pa[t][:, c], a_val[t][:, c], g1[t][:, c], ALU.subtract)
+
+        def diff2(t, c=slice(0, S)):
+            nc.vector.tensor_tensor(pb[t][:, c], g2[t][:, c], a_val[t][:, c], ALU.subtract)
+
+        def floor_a(t, c=slice(0, S)):
+            nc.vector.scalar_tensor_tensor(low[t][:, c], pb[t][:, c], 0.0, pa[t][:, c], ALU.min, ALU.max)
+
+        def ceil_a(t, c=slice(0, S)):
+            nc.vector.scalar_tensor_tensor(z_planes[:, t, c], pb[t][:, c], 0.0, low[t][:, c], ALU.max, ALU.min)
 
         def limit_a(t):
-            pa = sb(f"pa_{t}", [P, S], F32)
-            pb = sb(f"pb_{t}", [P, S], F32)
-            low = sb(f"low_{t}", [P, S], F32)
-            for c in cols:
-                nc.vector.tensor_tensor(pa[:, c], a_val[t][:, c], g1[t][:, c], ALU.subtract)
-                nc.vector.tensor_tensor(pb[:, c], g2[t][:, c], a_val[t][:, c], ALU.subtract)
-            for c in cols:
-                nc.vector.scalar_tensor_tensor(low[:, c], pb[:, c], 0.0, pa[:, c], ALU.min, ALU.max)
-            for c in cols:
-                nc.vector.scalar_tensor_tensor(z_planes[:, t, c], pb[:, c], 0.0, low[:, c], ALU.max, ALU.min)
+            if t > 0:
+                diff1(t)
+                floor_a(t - 1)
+                diff2(t)
+                ceil_a(t - 1)
+            else:
+                diff1(t)
+                diff2(t)
+            if t == PACK - 1:
+                for c in cols:
+                    floor_a(t, c)
+                for c in cols:
+                    ceil_a(t, c)
 
         CH = CHUNKS
         b_gain = [sb(f"b_gain{t}", [P, V], F32) for t in range(PACK)]
@@ -170,10 +200,12 @@ def tile_picked_kqminmodlerphopg_none_p_kernel(
         gate_b = [sb(f"gate_b{h}", [P, PACK, n], F32) for h, (lo, n) in enumerate(CH)]
 
         def open_gain(t):
-            nc.scalar.activation(b_gain[t][:], b_ps[t][:], ACT.Copy, scale=gb_sb[:, t : t + 1])
+            for acc, c in b_ps[t]:
+                nc.scalar.activation(b_gain[t][:, c], acc[:], ACT.Copy, scale=gb_sb[:, t : t + 1])
 
         def open_sig(t):
-            nc.scalar.activation(b_sig[t][:], b_ps[t][:], ACT.Sigmoid)
+            for acc, c in b_ps[t]:
+                nc.scalar.activation(b_sig[t][:, c], acc[:], ACT.Sigmoid)
 
         def near_b(ts, h, on_vector=False):
             lo, n = CH[h]
@@ -211,7 +243,7 @@ def tile_picked_kqminmodlerphopg_none_p_kernel(
             return quantize(f"z2_q{h}_{lo}", grouped[:].rearrange("p c t -> p (c t)"))
 
         s_val = [sb(f"s_val{t}", [P, V], F32) for t in range(PACK)]
-        s_sig = [sb(f"s_sig{t}", [P, V], F32) for t in range(PACK)]
+        s_sig = [sb(f"s_sig{t}", [P, WIDE], F32) for t in range(PACK)]
 
         def scores(zq, z2q, lo, n, bank0):
             accs = []
@@ -234,23 +266,16 @@ def tile_picked_kqminmodlerphopg_none_p_kernel(
             open_val_s(sc, t)
 
         out_rows = out.rearrange("(m t) v -> t m v", t=PACK)
-        st = [sb(f"st{t}", [P, V], F32) for t in range(PACK)]
+        st = [sb(f"st{t}", [P, WIDE if t < PACK - 1 else V], F32) for t in range(PACK)]
         hop = [sb(f"hop{t}", [P, V], F32) for t in range(PACK)]
         res = [sb(f"res{t}", [P, V], F32) for t in range(PACK)]
 
-        def gate(t):
-            for h in range(2):
-                nc.vector.tensor_tensor(
-                    st[t][:, cols[h]], s_sig[t][:].indirect(entries(l_n6, h * HALF, HALF)), s_val[t][:, cols[h]], ALU.mult
-                )
+        def gate(t, pieces=((0, V),)):
+            for lo, n in pieces:
+                c = slice(lo, lo + n)
+                nc.vector.tensor_tensor(st[t][:, c], s_sig[t][:].indirect(entries(l_n6, lo, n)), s_val[t][:, c], ALU.mult)
 
-        def gate_through(t):
-            for h in range(2):
-                nc.scalar.activation(s_sig[t][:, cols[h]], s_val[t][:].indirect(entries(l_n6, h * HALF, HALF)), ACT.Sigmoid)
-            for h in range(2):
-                nc.vector.tensor_tensor(st[t][:, cols[h]], s_sig[t][:, cols[h]], s_val[t][:, cols[h]], ALU.mult)
-
-        def hop_s(t, pieces=((0, HALF), (HALF, HALF)), v_fetch=()):
+        def hop_s(t, pieces=((0, V),), v_fetch=()):
             for lo, n in pieces:
                 fetch(lo in v_fetch, hop[t][:, lo : lo + n], st[t], l_n7, lo, n)
 
@@ -261,22 +286,22 @@ def tile_picked_kqminmodlerphopg_none_p_kernel(
                 nc.sync.dma_start(out_rows[t][:, c], res[t][:, c])
 
         z_grp = sb("z_grp", [P, PACK, P, PACK], BF16)
-        w2_grp = cast_weight("w2", w2_raw, 0)
+        w2_grp = cast_weight("w2", w2_raw, HALF)
         xb_s = pick_scales("xb", l_two)
-        xa_s = pick_scales("xa", l_offs)
-        xb = (pick_words("xb", l_two), xb_s)
         w2_q = quantize_weight("w2", w2_grp)
-        b_ps = project("w2", w2_q, xb, 0)
+        xb = (pick_words("xb", l_two, ((0, HALF), (HALF, HALF))), xb_s)
+        b_ps = project("w2", w2_q, xb, 0, 2 * PACK - 1)
+        xa_s = pick_scales("xa", l_offs)
         xa = (pick_words("xa", l_offs), xa_s)
         w1_grp = cast_weight("w1", w1_raw, H)
         w1_q = quantize_weight("w1", w1_grp)
-        a_ps = project("w1", w1_q, xa, PACK)
         open_sig(0)
         open_gain(0)
         near_b([0], 0)
         open_gain(1)
         near_b([1], 0)
         open_sig(1)
+        a_ps = project("w1", w1_q, xa, PACK)
         step_b([0, 1], 0)
         move_b([0, 1], 0)
         open_gain(2)
@@ -293,11 +318,13 @@ def tile_picked_kqminmodlerphopg_none_p_kernel(
         limit_a(0)
         fetch_a(2)
         limit_a(1)
-        near_b([0, 1], 1, True)
+        near_b([0], 1, True)
         fetch_a(3)
         limit_a(2)
         limit_a(3)
 
+        near_b([1], 1)
+        fetch_b(far, b_gain, l_n5, [1], 1)
         fetch_b(gate_b, b_sig, l_n4, [0, 1], 1)
         near_b([2, 3], 1)
         fetch_b(far, b_gain, l_n5, [2, 3], 1)
@@ -305,7 +332,8 @@ def tile_picked_kqminmodlerphopg_none_p_kernel(
         deal(nc.vector.tensor_copy, z_grp, 0, z_planes[:])
         zq = quantize("z_q", z_grp[:].rearrange("p t m j -> p (t m j)"))
         s0 = scores(zq, z2q0, 0, HALF, 0)
-        step_b([0, 1], 1, True)
+        step_b([0], 1, True)
+        step_b([1], 1, False)
         move_b([0, 1], 1, False)
         step_b([2, 3], 1, False)
         move_b([2, 3], 1, False)
@@ -313,18 +341,19 @@ def tile_picked_kqminmodlerphopg_none_p_kernel(
             open_s(s0, t)
         s1 = scores(zq, quant_b(1, 0, close_b(1)), HALF, HALF, PACK)
         open_s(s1, 0)
-        open_s(s1, 1)
-        gate(0)
+        open_val_s(s1, 1, True)
+        open_sig_s(s1, 1)
+        gate(0, ((0, HALF), (HALF, HALF)))
         open_s(s1, 2)
-        hop_s(0)
         gate(1)
+        hop_s(0)
         open_s(s1, 3)
         finish(0)
-        hop_s(1)
         gate(2)
+        hop_s(1)
         finish(1)
-        hop_s(2)
         gate(3)
+        hop_s(2)
         finish(2)
         hop_s(3, ((0, HALF), (HALF, P), (HALF + P, P)))
         finish(3, ((0, HALF), (HALF, P), (HALF + P, P)))

@@ -3,7 +3,7 @@ from contextlib import ExitStack
 import concourse.mybir as mybir
 
 K, T, S, V, H = 512, 2048, 512, 512, 512
-FLOPS = 3 * 2 * 512 * 512 * 512
+FLOPS = 2 * K * H * S + 2 * K * H * V + 2 * H * S * V
 
 F32 = mybir.dt.float32
 BF16 = mybir.dt.bfloat16
@@ -17,8 +17,14 @@ ACT = mybir.ActivationFunctionType
 
 P = 128
 PACK = 4
+LAST = PACK - 1
 HALF = 256
-CHUNKS = [(0, 256), (256, 256)]
+SCORE_SCALE = 0.0625
+WIDE = 2 * S
+WHOLE = ((0, S),)
+HALVES = ((0, HALF), (HALF, HALF))
+SHRINKING = ((0, HALF), (HALF, P), (HALF + P, P))
+COLS = (slice(0, HALF), slice(HALF, V))
 
 
 def tile_picked_kqminmodlerphopg_none_p_kernel(
@@ -29,19 +35,25 @@ def tile_picked_kqminmodlerphopg_none_p_kernel(
         keep = ctx.enter_context(tc.tile_pool(name="keep", bufs=1))
         psum = ctx.enter_context(tc.psum_pool(name="psum", bufs=1))
 
-        def sb(name, shape, dtype, tag=None):
-            return keep.tile(shape, dtype, name=name, tag=tag or name, align_bytes=64)
+        def sb(name, shape, dtype):
+            return keep.tile(shape, dtype, name=name, align_bytes=64)
+
+        def row_tiles(name, width):
+            return [sb(f"{name}{t}", [P, width], F32) for t in range(PACK)]
+
+        def half_tile(name):
+            return sb(name, [P, PACK, HALF], F32)
+
+        def bank(name, number, width):
+            return psum.tile([P, width], F32, name=name, tag=f"bank{number}")
 
         def load_list(name, src):
             tile = sb(name, [P, S // 16], U16)
             nc.sync.dma_start(tile[:], src)
             return tile
 
-        def entries(lst, lo, n):
-            return lst[:, lo // 16 : (lo + n) // 16]
-
         def load_weight(name, w):
-            raw = sb(f"{name}_raw", [P, PACK, H], F32)
+            raw = sb(name, [P, PACK, H], F32)
             nc.sync.dma_start(raw[:], w.rearrange("(p j) c -> p j c", j=PACK))
             return raw
 
@@ -53,14 +65,14 @@ def tile_picked_kqminmodlerphopg_none_p_kernel(
         x_sc = sb("x_sc", [P, T], U8)
         nc.vector.memset(x_sc[:].bitcast(I32), 0)
         l_two = load_list("l_two", two)
-        w2_raw = load_weight("w2", w2)
+        w2_raw = load_weight("w2_raw", w2)
         for q in range(4):
             nc.sync.dma_start(x_sc[32 * q : 32 * q + 4, :].bitcast(I32), x_scales[0, 4 * q : 4 * q + 4, :].bitcast(I32))
         gb_sb = load_gain("gb_sb", gb)
         x_w = sb("x_w", [P, T], U32)
         nc.sync.dma_start(x_w[:].bitcast(I32), x_words[0].rearrange("p n t -> p (n t)").bitcast(I32))
         l_offs = load_list("l_offs", offs)
-        w1_raw = load_weight("w1", w1)
+        w1_raw = load_weight("w1_raw", w1)
         l_n3 = load_list("l_n3", n3)
         l_n5 = load_list("l_n5", n5)
         l_n4 = load_list("l_n4", n4)
@@ -70,134 +82,104 @@ def tile_picked_kqminmodlerphopg_none_p_kernel(
         l_n6 = load_list("l_n6", n6)
         l_n7 = load_list("l_n7", n7)
 
-        def deal(copy, grouped, m0, planes):
+        def looked_up(window, lst, lo=0, n=S):
+            return window[:].indirect(lst[:, lo // 16 : (lo + n) // 16])
+
+        def scalar_fetch(dst, window, lst, lo=0, n=S):
+            nc.scalar.activation(dst, looked_up(window, lst, lo, n), ACT.Copy)
+
+        def deal(copy, dealt, m0, planes):
             count = planes.shape[2] // PACK
             copy(
-                grouped[:, :, m0 : m0 + count, :].rearrange("p (u i) m j -> p u m j i", i=2),
+                dealt[:, :, m0 : m0 + count, :].rearrange("p (u i) m j -> p u m j i", i=2),
                 planes.rearrange("p j (m u i) -> p u m j i", u=2, i=2),
             )
 
-        def pick_scales(name, lst):
-            scales = sb(f"{name}_s", [P, S], U8)
-            nc.vector.tensor_copy(scales[:], x_sc[:].indirect(lst[:]))
-            return scales
+        def dealt_tile(name):
+            return sb(name, [P, PACK, P, PACK], BF16)
 
-        def pick_words(name, lst, pieces=((0, S),)):
-            words = sb(f"{name}_w", [P, S], U32)
-            for lo, n in pieces:
-                nc.vector.tensor_copy(words[:, lo : lo + n], x_w[:].indirect(entries(lst, lo, n)))
-            return words
-
-        def quantize(name, grouped_flat):
-            width = grouped_flat.shape[1] // PACK
+        def quantize(name, values):
+            width = values.shape[1] // PACK
             words = sb(f"{name}_w", [P, width], U32)
             scales = sb(f"{name}_s", [P, width], U8)
-            nc.vector.quantize_mx(out=words[:].bitcast(FP8X4), scales=scales[:], in_=grouped_flat)
+            nc.vector.quantize_mx(out=words[:].bitcast(FP8X4), scales=scales[:], in_=values)
             return words, scales
 
-        def mx(acc, lhs, lhs_cols, rhs, rhs_cols=slice(None)):
+        def quantize_dealt(name, dealt):
+            return quantize(name, dealt[:].rearrange("p t m j -> p (t m j)"))
+
+        def pick_scales(name, lst):
+            scales = sb(name, [P, S], U8)
+            nc.vector.tensor_copy(scales[:], looked_up(x_sc, lst))
+            return scales
+
+        def pick_words(name, lst, pieces):
+            words = sb(name, [P, S], U32)
+            for lo, n in pieces:
+                nc.vector.tensor_copy(words[:, lo : lo + n], looked_up(x_w, lst, lo, n))
+            return words
+
+        def product(acc, stationary, t, moving, cols=slice(None)):
+            rows = slice(t * P, (t + 1) * P)
             nc.tensor.matmul_mx(
-                out=acc,
-                lhsT=lhs[0][:, lhs_cols].bitcast(FP8X4),
-                lhsT_scale=lhs[1][:, lhs_cols],
-                rhs=rhs[0][:, rhs_cols].bitcast(FP8X4),
-                rhs_scale=rhs[1][:, rhs_cols],
+                out=acc[:],
+                lhsT=stationary[0][:, rows].bitcast(FP8X4),
+                lhsT_scale=stationary[1][:, rows],
+                rhs=moving[0][:, cols].bitcast(FP8X4),
+                rhs_scale=moving[1][:, cols],
                 start=True,
                 stop=True,
             )
+            return acc
 
-        def cast_weight(name, raw, vector_cols):
-            grouped = sb(f"{name}_grp", [P, PACK, P, PACK], BF16)
-            if vector_cols:
-                deal(nc.vector.tensor_copy, grouped, 0, raw[:, :, :vector_cols])
-            if vector_cols < H:
-                deal(nc.scalar.copy, grouped, vector_cols // PACK, raw[:, :, vector_cols:])
-            return grouped
+        w2_dealt = dealt_tile("w2_dealt")
+        deal(nc.vector.tensor_copy, w2_dealt, 0, w2_raw[:, :, COLS[0]])
+        deal(nc.scalar.copy, w2_dealt, HALF // PACK, w2_raw[:, :, COLS[1]])
+        xb_scales = pick_scales("xb_s", l_two)
+        w2_q = quantize_dealt("w2_q", w2_dealt)
+        xb = (pick_words("xb_w", l_two, HALVES), xb_scales)
+        b_ps = [[(product(bank(f"b0_{h}", (0, 2 * PACK - 1)[h], HALF), w2_q, 0, xb, COLS[h]), COLS[h]) for h in range(2)]]
+        for t in range(1, PACK):
+            b_ps.append([(product(bank(f"b{t}", t, V), w2_q, t, xb), slice(0, V))])
+        xa_scales = pick_scales("xa_s", l_offs)
+        xa = (pick_words("xa_w", l_offs, WHOLE), xa_scales)
+        w1_dealt = dealt_tile("w1_dealt")
+        deal(nc.vector.tensor_copy, w1_dealt, 0, w1_raw[:])
+        w1_q = quantize_dealt("w1_q", w1_dealt)
 
-        def quantize_weight(name, grouped):
-            return [quantize(f"{name}_q{t}", grouped[:, t, :, :].rearrange("p m j -> p (m j)")) for t in range(PACK)]
-
-        def project(name, wq, picked, bank0, spare_bank=None):
-            accs = []
-            for t in range(PACK):
-                if t == 0 and spare_bank is not None:
-                    parts = []
-                    for h, bank in enumerate((bank0, spare_bank)):
-                        acc = psum.tile([P, HALF], F32, name=f"{name}_acc{t}_{h}", tag=f"bank{bank}")
-                        c = slice(h * HALF, (h + 1) * HALF)
-                        mx(acc[:], wq[t], slice(0, P), picked, c)
-                        parts.append((acc, c))
-                else:
-                    acc = psum.tile([P, S], F32, name=f"{name}_acc{t}", tag=f"bank{bank0 + t}")
-                    mx(acc[:], wq[t], slice(0, P), picked)
-                    parts = [(acc, slice(0, S))]
-                accs.append(parts)
-            return accs
-
-        def fetch(on_vector, dst, window, lst, lo, n):
-            if on_vector:
-                nc.vector.tensor_copy(dst, window[:].indirect(entries(lst, lo, n)))
-            else:
-                nc.scalar.activation(dst, window[:].indirect(entries(lst, lo, n)), ACT.Copy)
-
-        def scaled(on_vector, dst, acc, gain):
-            if on_vector:
-                nc.vector.tensor_scalar(dst, acc, gain, None, ALU.mult)
-            else:
-                nc.scalar.activation(dst, acc, ACT.Copy, scale=gain)
-
-        WIDE = 2 * S
+        a_val = row_tiles("a_val", WIDE)
+        a_n1, a_n2 = row_tiles("a_n1_", S), row_tiles("a_n2_", S)
+        pa, pb, floored = row_tiles("pa", S), row_tiles("pb", S), row_tiles("floored", S)
         z_planes = sb("z_planes", [P, PACK, S], F32)
-        cols = [slice(h * HALF, (h + 1) * HALF) for h in range(2)]
-        a_val = [sb(f"a{t}", [P, WIDE], F32) for t in range(PACK)]
-        g1 = [sb(f"g1_{t}", [P, S], F32) for t in range(PACK)]
-        g2 = [sb(f"g2_{t}", [P, S], F32) for t in range(PACK)]
 
         def fetch_a(t):
-            for acc, c in a_ps[t]:
-                scaled(False, a_val[t][:, c], acc[:], ga_sb[:, t : t + 1])
-            fetch(False, g1[t][:], a_val[t], l_n1, 0, S)
-            fetch(False, g2[t][:], a_val[t], l_n2, 0, S)
+            nc.scalar.activation(a_val[t][:, :S], a_ps[t][:], ACT.Copy, scale=ga_sb[:, t : t + 1])
+            scalar_fetch(a_n1[t][:], a_val[t], l_n1)
+            scalar_fetch(a_n2[t][:], a_val[t], l_n2)
 
-        pa = [sb(f"pa_{t}", [P, S], F32) for t in range(PACK)]
-        pb = [sb(f"pb_{t}", [P, S], F32) for t in range(PACK)]
-        low = [sb(f"low_{t}", [P, S], F32) for t in range(PACK)]
+        def make_pa(t):
+            nc.vector.tensor_tensor(pa[t][:], a_val[t][:, :S], a_n1[t][:], ALU.subtract)
 
-        def diff1(t, c=slice(0, S)):
-            nc.vector.tensor_tensor(pa[t][:, c], a_val[t][:, c], g1[t][:, c], ALU.subtract)
+        def make_pb(t):
+            nc.vector.tensor_tensor(pb[t][:], a_n2[t][:], a_val[t][:, :S], ALU.subtract)
 
-        def diff2(t, c=slice(0, S)):
-            nc.vector.tensor_tensor(pb[t][:, c], g2[t][:, c], a_val[t][:, c], ALU.subtract)
+        def clamp_below(t, c=slice(0, S)):
+            nc.vector.scalar_tensor_tensor(floored[t][:, c], pb[t][:, c], 0.0, pa[t][:, c], ALU.min, ALU.max)
 
-        def floor_a(t, c=slice(0, S)):
-            nc.vector.scalar_tensor_tensor(low[t][:, c], pb[t][:, c], 0.0, pa[t][:, c], ALU.min, ALU.max)
+        def clamp_above(t, c=slice(0, S)):
+            nc.vector.scalar_tensor_tensor(z_planes[:, t, c], pb[t][:, c], 0.0, floored[t][:, c], ALU.max, ALU.min)
 
-        def ceil_a(t, c=slice(0, S)):
-            nc.vector.scalar_tensor_tensor(z_planes[:, t, c], pb[t][:, c], 0.0, low[t][:, c], ALU.max, ALU.min)
+        def differences_with_clamps(t):
+            make_pa(t)
+            clamp_below(t - 1)
+            make_pb(t)
+            clamp_above(t - 1)
 
-        def limit_a(t):
-            if t > 0:
-                diff1(t)
-                floor_a(t - 1)
-                diff2(t)
-                ceil_a(t - 1)
-            else:
-                diff1(t)
-                diff2(t)
-            if t == PACK - 1:
-                for c in cols:
-                    floor_a(t, c)
-                for c in cols:
-                    ceil_a(t, c)
-
-        CH = CHUNKS
-        b_gain = [sb(f"b_gain{t}", [P, V], F32) for t in range(PACK)]
-        b_sig = [sb(f"b_sig{t}", [P, V], F32) for t in range(PACK)]
-        near = [sb(f"near{h}", [P, PACK, n], F32) for h, (lo, n) in enumerate(CH)]
-        step = [sb(f"step{h}", [P, PACK, n], F32) for h, (lo, n) in enumerate(CH)]
-        move = [sb(f"move{h}", [P, PACK, n], F32) for h, (lo, n) in enumerate(CH)]
-        far = [sb(f"far{h}", [P, PACK, n], F32) for h, (lo, n) in enumerate(CH)]
-        gate_b = [sb(f"gate_b{h}", [P, PACK, n], F32) for h, (lo, n) in enumerate(CH)]
+        b_gain, b_sig = row_tiles("b_gain", V), row_tiles("b_sig", V)
+        near = [half_tile(f"near{h}") for h in range(2)]
+        step = [half_tile(f"step{h}") for h in range(2)]
+        move = [half_tile(f"move{h}") for h in range(2)]
+        far_late, sig_late = half_tile("far_late"), half_tile("sig_late")
 
         def open_gain(t):
             for acc, c in b_ps[t]:
@@ -207,153 +189,130 @@ def tile_picked_kqminmodlerphopg_none_p_kernel(
             for acc, c in b_ps[t]:
                 nc.scalar.activation(b_sig[t][:, c], acc[:], ACT.Sigmoid)
 
-        def near_b(ts, h, on_vector=False):
-            lo, n = CH[h]
-            for t in ts:
-                fetch(on_vector, near[h][:, t, :], b_gain[t], l_n3, lo, n)
+        def fetch_half(dst, windows, lst, tiles, h):
+            for t in tiles:
+                scalar_fetch(dst[:, t, :], windows[t], lst, *HALVES[h])
 
-        def fetch_b(dst, window, lst, ts, h):
-            lo, n = CH[h]
-            for t in ts:
-                fetch(False, dst[h][:, t, :], window[t], lst, lo, n)
+        def fused_step(t, h):
+            far = looked_up(b_gain[t], l_n5, *HALVES[h])
+            nc.vector.tensor_tensor(step[h][:, t, :], far, near[h][:, t, :], ALU.subtract)
 
-        def step_b(ts, h, fused=True):
-            lo, n = CH[h]
-            for t in ts:
-                far_t = b_gain[t][:].indirect(entries(l_n5, lo, n)) if fused else far[h][:, t, :]
-                nc.vector.tensor_tensor(step[h][:, t, :], far_t, near[h][:, t, :], ALU.subtract)
+        def fused_first_half(tiles):
+            for t in tiles:
+                fused_step(t, 0)
+            for t in tiles:
+                sig = looked_up(b_sig[t], l_n4, *HALVES[0])
+                nc.vector.tensor_tensor(move[0][:, t, :], sig, step[0][:, t, :], ALU.mult)
 
-        def move_b(ts, h, fused=True):
-            lo, n = CH[h]
-            for t in ts:
-                gate_t = b_sig[t][:].indirect(entries(l_n4, lo, n)) if fused else gate_b[h][:, t, :]
-                nc.vector.tensor_tensor(move[h][:, t, :], gate_t, step[h][:, t, :], ALU.mult)
+        def late_step(tiles):
+            nc.vector.tensor_tensor(step[1][:, tiles, :], far_late[:, tiles, :], near[1][:, tiles, :], ALU.subtract)
 
-        def close_b(h, lo=0, n=HALF):
-            grouped = sb(f"z2_grp{h}_{lo}", [P, n, PACK], BF16)
+        def late_move(tiles):
+            nc.vector.tensor_tensor(move[1][:, tiles, :], sig_late[:, tiles, :], step[1][:, tiles, :], ALU.mult)
+
+        def quantize_z2(h):
+            z2 = sb(f"z2_{h}", [P, HALF, PACK], BF16)
             nc.vector.tensor_tensor(
-                grouped[:].rearrange("p (c i) t -> p c t i", i=2),
-                near[h][:, :, lo : lo + n].rearrange("p t (c i) -> p c t i", i=2),
-                move[h][:, :, lo : lo + n].rearrange("p t (c i) -> p c t i", i=2),
+                z2[:].rearrange("p (c i) t -> p c t i", i=2),
+                near[h][:].rearrange("p t (c i) -> p c t i", i=2),
+                move[h][:].rearrange("p t (c i) -> p c t i", i=2),
                 ALU.add,
             )
-            return grouped
+            return quantize(f"z2_q{h}", z2[:].rearrange("p c t -> p (c t)"))
 
-        def quant_b(h, lo, grouped):
-            return quantize(f"z2_q{h}_{lo}", grouped[:].rearrange("p c t -> p (c t)"))
-
-        s_val = [sb(f"s_val{t}", [P, V], F32) for t in range(PACK)]
-        s_sig = [sb(f"s_sig{t}", [P, WIDE], F32) for t in range(PACK)]
-
-        def scores(zq, z2q, lo, n, bank0):
-            accs = []
-            for t in range(PACK):
-                acc = psum.tile([P, n], F32, name=f"s_acc{lo}_{t}", tag=f"bank{bank0 + t}")
-                mx(acc[:], zq, slice(t * P, (t + 1) * P), z2q)
-                accs.append(acc)
-            return accs, lo, n
-
-        def open_sig_s(sc, t):
-            accs, lo, n = sc
-            nc.scalar.activation(s_sig[t][:, lo : lo + n], accs[t][:], ACT.Sigmoid, scale=0.0625)
-
-        def open_val_s(sc, t, on_vector=False):
-            accs, lo, n = sc
-            scaled(on_vector, s_val[t][:, lo : lo + n], accs[t][:], 0.0625)
-
-        def open_s(sc, t):
-            open_sig_s(sc, t)
-            open_val_s(sc, t)
-
+        s_val, s_sig = row_tiles("s_val", V), row_tiles("s_sig", WIDE)
+        st = [sb(f"st{t}", [P, V if t == LAST else WIDE], F32) for t in range(PACK)]
+        st_n7, result = row_tiles("st_n7_", V), row_tiles("result", V)
         out_rows = out.rearrange("(m t) v -> t m v", t=PACK)
-        st = [sb(f"st{t}", [P, WIDE if t < PACK - 1 else V], F32) for t in range(PACK)]
-        hop = [sb(f"hop{t}", [P, V], F32) for t in range(PACK)]
-        res = [sb(f"res{t}", [P, V], F32) for t in range(PACK)]
 
-        def gate(t, pieces=((0, V),)):
+        def scores(z2_q, h):
+            return [product(bank(f"s{h}_{t}", PACK * h + t, HALF), z_q, t, z2_q) for t in range(PACK)]
+
+        def open_score_sig(t, h):
+            nc.scalar.activation(s_sig[t][:, COLS[h]], s_ps[h][t][:], ACT.Sigmoid, scale=SCORE_SCALE)
+
+        def open_scores(t, h):
+            open_score_sig(t, h)
+            nc.scalar.activation(s_val[t][:, COLS[h]], s_ps[h][t][:], ACT.Copy, scale=SCORE_SCALE)
+
+        def gate(t, pieces=WHOLE):
             for lo, n in pieces:
                 c = slice(lo, lo + n)
-                nc.vector.tensor_tensor(st[t][:, c], s_sig[t][:].indirect(entries(l_n6, lo, n)), s_val[t][:, c], ALU.mult)
+                nc.vector.tensor_tensor(st[t][:, c], looked_up(s_sig[t], l_n6, lo, n), s_val[t][:, c], ALU.mult)
 
-        def hop_s(t, pieces=((0, V),), v_fetch=()):
+        def fetch_st(t, pieces=WHOLE):
             for lo, n in pieces:
-                fetch(lo in v_fetch, hop[t][:, lo : lo + n], st[t], l_n7, lo, n)
+                scalar_fetch(st_n7[t][:, lo : lo + n], st[t], l_n7, lo, n)
 
-        def finish(t, pieces=((0, V),)):
+        def finish(t, pieces=WHOLE):
             for lo, n in pieces:
                 c = slice(lo, lo + n)
-                nc.vector.tensor_tensor(res[t][:, c], st[t][:, c], hop[t][:, c], ALU.subtract)
-                nc.sync.dma_start(out_rows[t][:, c], res[t][:, c])
+                nc.vector.tensor_tensor(result[t][:, c], st[t][:, c], st_n7[t][:, c], ALU.subtract)
+                nc.sync.dma_start(out_rows[t][:, c], result[t][:, c])
 
-        z_grp = sb("z_grp", [P, PACK, P, PACK], BF16)
-        w2_grp = cast_weight("w2", w2_raw, HALF)
-        xb_s = pick_scales("xb", l_two)
-        w2_q = quantize_weight("w2", w2_grp)
-        xb = (pick_words("xb", l_two, ((0, HALF), (HALF, HALF))), xb_s)
-        b_ps = project("w2", w2_q, xb, 0, 2 * PACK - 1)
-        xa_s = pick_scales("xa", l_offs)
-        xa = (pick_words("xa", l_offs), xa_s)
-        w1_grp = cast_weight("w1", w1_raw, H)
-        w1_q = quantize_weight("w1", w1_grp)
         open_sig(0)
-        open_gain(0)
-        near_b([0], 0)
-        open_gain(1)
-        near_b([1], 0)
+        for t in (0, 1):
+            open_gain(t)
+            fetch_half(near[0], b_gain, l_n3, [t], 0)
         open_sig(1)
-        a_ps = project("w1", w1_q, xa, PACK)
-        step_b([0, 1], 0)
-        move_b([0, 1], 0)
-        open_gain(2)
-        near_b([2], 0)
-        open_gain(3)
-        near_b([3], 0)
-        open_sig(2)
-        open_sig(3)
+        a_ps = [product(bank(f"a{t}", PACK + t, S), w1_q, t, xa) for t in range(PACK)]
+        fused_first_half((0, 1))
+        for t in (2, 3):
+            open_gain(t)
+            fetch_half(near[0], b_gain, l_n3, [t], 0)
+        for t in (2, 3):
+            open_sig(t)
         fetch_a(0)
-        step_b([2, 3], 0)
-        move_b([2, 3], 0)
+        fused_first_half((2, 3))
         fetch_a(1)
-        z2q0 = quant_b(0, 0, close_b(0))
-        limit_a(0)
-        fetch_a(2)
-        limit_a(1)
-        near_b([0], 1, True)
-        fetch_a(3)
-        limit_a(2)
-        limit_a(3)
+        z2_first = quantize_z2(0)
 
-        near_b([1], 1)
-        fetch_b(far, b_gain, l_n5, [1], 1)
-        fetch_b(gate_b, b_sig, l_n4, [0, 1], 1)
-        near_b([2, 3], 1)
-        fetch_b(far, b_gain, l_n5, [2, 3], 1)
-        fetch_b(gate_b, b_sig, l_n4, [2, 3], 1)
-        deal(nc.vector.tensor_copy, z_grp, 0, z_planes[:])
-        zq = quantize("z_q", z_grp[:].rearrange("p t m j -> p (t m j)"))
-        s0 = scores(zq, z2q0, 0, HALF, 0)
-        step_b([0], 1, True)
-        step_b([1], 1, False)
-        move_b([0, 1], 1, False)
-        step_b([2, 3], 1, False)
-        move_b([2, 3], 1, False)
+        make_pa(0)
+        make_pb(0)
+        fetch_a(2)
+        differences_with_clamps(1)
+        for t in (0, 1):
+            nc.vector.tensor_copy(near[1][:, t, :], looked_up(b_gain[t], l_n3, *HALVES[1]))
+        fetch_a(3)
+        differences_with_clamps(2)
+        differences_with_clamps(3)
+        for c in COLS:
+            clamp_below(LAST, c)
+        for c in COLS:
+            clamp_above(LAST, c)
+
+        fetch_half(far_late, b_gain, l_n5, [1], 1)
+        fetch_half(sig_late, b_sig, l_n4, [0, 1], 1)
+        fetch_half(near[1], b_gain, l_n3, [2, 3], 1)
+        fetch_half(far_late, b_gain, l_n5, [2, 3], 1)
+        fetch_half(sig_late, b_sig, l_n4, [2, 3], 1)
+        z_dealt = dealt_tile("z_dealt")
+        deal(nc.vector.tensor_copy, z_dealt, 0, z_planes[:])
+        z_q = quantize_dealt("z_q", z_dealt)
+        s_ps = [scores(z2_first, 0)]
+        fused_step(0, 1)
+        late_step(slice(1, 2))
+        late_move(slice(0, 2))
+        late_step(slice(2, PACK))
+        late_move(slice(2, PACK))
         for t in range(PACK):
-            open_s(s0, t)
-        s1 = scores(zq, quant_b(1, 0, close_b(1)), HALF, HALF, PACK)
-        open_s(s1, 0)
-        open_val_s(s1, 1, True)
-        open_sig_s(s1, 1)
-        gate(0, ((0, HALF), (HALF, HALF)))
-        open_s(s1, 2)
+            open_scores(t, 0)
+        s_ps.append(scores(quantize_z2(1), 1))
+
+        open_scores(0, 1)
+        nc.vector.tensor_scalar(s_val[1][:, COLS[1]], s_ps[1][1][:], SCORE_SCALE, None, ALU.mult)
+        open_score_sig(1, 1)
+        gate(0, HALVES)
+        open_scores(2, 1)
         gate(1)
-        hop_s(0)
-        open_s(s1, 3)
-        finish(0)
+        open_scores(3, 1)
+        fetch_st(0)
         gate(2)
-        hop_s(1)
-        finish(1)
+        fetch_st(1)
         gate(3)
-        hop_s(2)
+        finish(0)
+        fetch_st(2)
+        finish(1)
+        fetch_st(LAST, SHRINKING)
         finish(2)
-        hop_s(3, ((0, HALF), (HALF, P), (HALF + P, P)))
-        finish(3, ((0, HALF), (HALF, P), (HALF + P, P)))
+        finish(LAST, SHRINKING)

from contextlib import ExitStack

import concourse.mybir as mybir

K, T, S, V, H = 512, 2048, 512, 512, 512
FLOPS = 2 * K * H * S + 2 * K * H * V + 2 * H * S * V

F32 = mybir.dt.float32
BF16 = mybir.dt.bfloat16
U32 = mybir.dt.uint32
I32 = mybir.dt.int32
U16 = mybir.dt.uint16
U8 = mybir.dt.uint8
FP8X4 = mybir.dt.float8_e4m3fn_x4
ALU = mybir.AluOpType
ACT = mybir.ActivationFunctionType

P = 128
PACK = 4
LAST = PACK - 1
HALF = 256
SCORE_SCALE = 0.0625
WIDE = 2 * S
WHOLE = ((0, S),)
HALVES = ((0, HALF), (HALF, HALF))
SHRINKING = ((0, HALF), (HALF, P), (HALF + P, P))
COLS = (slice(0, HALF), slice(HALF, V))


def tile_picked_kqminmodlerphopg_none_p_kernel(
    tc, x_words, x_scales, w1, w2, ga, gb, offs, two, n1, n2, n3, n4, n5, n6, n7, out
):
    nc = tc.nc
    with ExitStack() as ctx:
        keep = ctx.enter_context(tc.tile_pool(name="keep", bufs=1))
        psum = ctx.enter_context(tc.psum_pool(name="psum", bufs=1))

        def sb(name, shape, dtype):
            return keep.tile(shape, dtype, name=name, align_bytes=64)

        def row_tiles(name, width):
            return [sb(f"{name}{t}", [P, width], F32) for t in range(PACK)]

        def half_tile(name):
            return sb(name, [P, PACK, HALF], F32)

        def bank(name, number, width):
            return psum.tile([P, width], F32, name=name, tag=f"bank{number}")

        def load_list(name, src):
            tile = sb(name, [P, S // 16], U16)
            nc.sync.dma_start(tile[:], src)
            return tile

        def load_weight(name, w):
            raw = sb(name, [P, PACK, H], F32)
            nc.sync.dma_start(raw[:], w.rearrange("(p j) c -> p j c", j=PACK))
            return raw

        def load_gain(name, g):
            tile = sb(name, [P, PACK], F32)
            nc.sync.dma_start(tile[:], g.rearrange("(p t) o -> p (t o)", t=PACK))
            return tile

        x_sc = sb("x_sc", [P, T], U8)
        nc.vector.memset(x_sc[:].bitcast(I32), 0)
        l_two = load_list("l_two", two)
        w2_raw = load_weight("w2_raw", w2)
        for q in range(4):
            nc.sync.dma_start(x_sc[32 * q : 32 * q + 4, :].bitcast(I32), x_scales[0, 4 * q : 4 * q + 4, :].bitcast(I32))
        gb_sb = load_gain("gb_sb", gb)
        x_w = sb("x_w", [P, T], U32)
        nc.sync.dma_start(x_w[:].bitcast(I32), x_words[0].rearrange("p n t -> p (n t)").bitcast(I32))
        l_offs = load_list("l_offs", offs)
        w1_raw = load_weight("w1_raw", w1)
        l_n3 = load_list("l_n3", n3)
        l_n5 = load_list("l_n5", n5)
        l_n4 = load_list("l_n4", n4)
        ga_sb = load_gain("ga_sb", ga)
        l_n1 = load_list("l_n1", n1)
        l_n2 = load_list("l_n2", n2)
        l_n6 = load_list("l_n6", n6)
        l_n7 = load_list("l_n7", n7)

        def looked_up(window, lst, lo=0, n=S):
            return window[:].indirect(lst[:, lo // 16 : (lo + n) // 16])

        def scalar_fetch(dst, window, lst, lo=0, n=S):
            nc.scalar.activation(dst, looked_up(window, lst, lo, n), ACT.Copy)

        def deal(copy, dealt, m0, planes):
            count = planes.shape[2] // PACK
            copy(
                dealt[:, :, m0 : m0 + count, :].rearrange("p (u i) m j -> p u m j i", i=2),
                planes.rearrange("p j (m u i) -> p u m j i", u=2, i=2),
            )

        def dealt_tile(name):
            return sb(name, [P, PACK, P, PACK], BF16)

        def quantize(name, values):
            width = values.shape[1] // PACK
            words = sb(f"{name}_w", [P, width], U32)
            scales = sb(f"{name}_s", [P, width], U8)
            nc.vector.quantize_mx(out=words[:].bitcast(FP8X4), scales=scales[:], in_=values)
            return words, scales

        def quantize_dealt(name, dealt):
            return quantize(name, dealt[:].rearrange("p t m j -> p (t m j)"))

        def pick_scales(name, lst):
            scales = sb(name, [P, S], U8)
            nc.vector.tensor_copy(scales[:], looked_up(x_sc, lst))
            return scales

        def pick_words(name, lst, pieces):
            words = sb(name, [P, S], U32)
            for lo, n in pieces:
                nc.vector.tensor_copy(words[:, lo : lo + n], looked_up(x_w, lst, lo, n))
            return words

        def product(acc, stationary, t, moving, cols=slice(None)):
            rows = slice(t * P, (t + 1) * P)
            nc.tensor.matmul_mx(
                out=acc[:],
                lhsT=stationary[0][:, rows].bitcast(FP8X4),
                lhsT_scale=stationary[1][:, rows],
                rhs=moving[0][:, cols].bitcast(FP8X4),
                rhs_scale=moving[1][:, cols],
                start=True,
                stop=True,
            )
            return acc

        w2_dealt = dealt_tile("w2_dealt")
        deal(nc.vector.tensor_copy, w2_dealt, 0, w2_raw[:, :, COLS[0]])
        deal(nc.scalar.copy, w2_dealt, HALF // PACK, w2_raw[:, :, COLS[1]])
        xb_scales = pick_scales("xb_s", l_two)
        w2_q = quantize_dealt("w2_q", w2_dealt)
        xb = (pick_words("xb_w", l_two, HALVES), xb_scales)
        b_ps = [[(product(bank(f"b0_{h}", (0, 2 * PACK - 1)[h], HALF), w2_q, 0, xb, COLS[h]), COLS[h]) for h in range(2)]]
        for t in range(1, PACK):
            b_ps.append([(product(bank(f"b{t}", t, V), w2_q, t, xb), slice(0, V))])
        xa_scales = pick_scales("xa_s", l_offs)
        xa = (pick_words("xa_w", l_offs, WHOLE), xa_scales)
        w1_dealt = dealt_tile("w1_dealt")
        deal(nc.vector.tensor_copy, w1_dealt, 0, w1_raw[:])
        w1_q = quantize_dealt("w1_q", w1_dealt)

        a_val = row_tiles("a_val", WIDE)
        a_n1, a_n2 = row_tiles("a_n1_", S), row_tiles("a_n2_", S)
        pa, pb, floored = row_tiles("pa", S), row_tiles("pb", S), row_tiles("floored", S)
        z_planes = sb("z_planes", [P, PACK, S], F32)

        def fetch_a(t):
            nc.scalar.activation(a_val[t][:, :S], a_ps[t][:], ACT.Copy, scale=ga_sb[:, t : t + 1])
            scalar_fetch(a_n1[t][:], a_val[t], l_n1)
            scalar_fetch(a_n2[t][:], a_val[t], l_n2)

        def make_pa(t):
            nc.vector.tensor_tensor(pa[t][:], a_val[t][:, :S], a_n1[t][:], ALU.subtract)

        def make_pb(t):
            nc.vector.tensor_tensor(pb[t][:], a_n2[t][:], a_val[t][:, :S], ALU.subtract)

        def clamp_below(t, c=slice(0, S)):
            nc.vector.scalar_tensor_tensor(floored[t][:, c], pb[t][:, c], 0.0, pa[t][:, c], ALU.min, ALU.max)

        def clamp_above(t, c=slice(0, S)):
            nc.vector.scalar_tensor_tensor(z_planes[:, t, c], pb[t][:, c], 0.0, floored[t][:, c], ALU.max, ALU.min)

        def differences_with_clamps(t):
            make_pa(t)
            clamp_below(t - 1)
            make_pb(t)
            clamp_above(t - 1)

        b_gain, b_sig = row_tiles("b_gain", V), row_tiles("b_sig", V)
        near = [half_tile(f"near{h}") for h in range(2)]
        step = [half_tile(f"step{h}") for h in range(2)]
        move = [half_tile(f"move{h}") for h in range(2)]
        far_late, sig_late = half_tile("far_late"), half_tile("sig_late")

        def open_gain(t):
            for acc, c in b_ps[t]:
                nc.scalar.activation(b_gain[t][:, c], acc[:], ACT.Copy, scale=gb_sb[:, t : t + 1])

        def open_sig(t):
            for acc, c in b_ps[t]:
                nc.scalar.activation(b_sig[t][:, c], acc[:], ACT.Sigmoid)

        def fetch_half(dst, windows, lst, tiles, h):
            for t in tiles:
                scalar_fetch(dst[:, t, :], windows[t], lst, *HALVES[h])

        def fused_step(t, h):
            far = looked_up(b_gain[t], l_n5, *HALVES[h])
            nc.vector.tensor_tensor(step[h][:, t, :], far, near[h][:, t, :], ALU.subtract)

        def fused_first_half(tiles):
            for t in tiles:
                fused_step(t, 0)
            for t in tiles:
                sig = looked_up(b_sig[t], l_n4, *HALVES[0])
                nc.vector.tensor_tensor(move[0][:, t, :], sig, step[0][:, t, :], ALU.mult)

        def late_step(tiles):
            nc.vector.tensor_tensor(step[1][:, tiles, :], far_late[:, tiles, :], near[1][:, tiles, :], ALU.subtract)

        def late_move(tiles):
            nc.vector.tensor_tensor(move[1][:, tiles, :], sig_late[:, tiles, :], step[1][:, tiles, :], ALU.mult)

        def quantize_z2(h):
            z2 = sb(f"z2_{h}", [P, HALF, PACK], BF16)
            nc.vector.tensor_tensor(
                z2[:].rearrange("p (c i) t -> p c t i", i=2),
                near[h][:].rearrange("p t (c i) -> p c t i", i=2),
                move[h][:].rearrange("p t (c i) -> p c t i", i=2),
                ALU.add,
            )
            return quantize(f"z2_q{h}", z2[:].rearrange("p c t -> p (c t)"))

        s_val, s_sig = row_tiles("s_val", V), row_tiles("s_sig", WIDE)
        st = [sb(f"st{t}", [P, V if t == LAST else WIDE], F32) for t in range(PACK)]
        st_n7, result = row_tiles("st_n7_", V), row_tiles("result", V)
        out_rows = out.rearrange("(m t) v -> t m v", t=PACK)

        def scores(z2_q, h):
            return [product(bank(f"s{h}_{t}", PACK * h + t, HALF), z_q, t, z2_q) for t in range(PACK)]

        def open_score_sig(t, h):
            nc.scalar.activation(s_sig[t][:, COLS[h]], s_ps[h][t][:], ACT.Sigmoid, scale=SCORE_SCALE)

        def open_scores(t, h):
            open_score_sig(t, h)
            nc.scalar.activation(s_val[t][:, COLS[h]], s_ps[h][t][:], ACT.Copy, scale=SCORE_SCALE)

        def gate(t, pieces=WHOLE):
            for lo, n in pieces:
                c = slice(lo, lo + n)
                nc.vector.tensor_tensor(st[t][:, c], looked_up(s_sig[t], l_n6, lo, n), s_val[t][:, c], ALU.mult)

        def fetch_st(t, pieces=WHOLE):
            for lo, n in pieces:
                scalar_fetch(st_n7[t][:, lo : lo + n], st[t], l_n7, lo, n)

        def finish(t, pieces=WHOLE):
            for lo, n in pieces:
                c = slice(lo, lo + n)
                nc.vector.tensor_tensor(result[t][:, c], st[t][:, c], st_n7[t][:, c], ALU.subtract)
                nc.sync.dma_start(out_rows[t][:, c], result[t][:, c])

        open_sig(0)
        for t in (0, 1):
            open_gain(t)
            fetch_half(near[0], b_gain, l_n3, [t], 0)
        open_sig(1)
        a_ps = [product(bank(f"a{t}", PACK + t, S), w1_q, t, xa) for t in range(PACK)]
        fused_first_half((0, 1))
        for t in (2, 3):
            open_gain(t)
            fetch_half(near[0], b_gain, l_n3, [t], 0)
        for t in (2, 3):
            open_sig(t)
        fetch_a(0)
        fused_first_half((2, 3))
        fetch_a(1)
        z2_first = quantize_z2(0)

        make_pa(0)
        make_pb(0)
        fetch_a(2)
        differences_with_clamps(1)
        for t in (0, 1):
            nc.vector.tensor_copy(near[1][:, t, :], looked_up(b_gain[t], l_n3, *HALVES[1]))
        fetch_a(3)
        differences_with_clamps(2)
        differences_with_clamps(3)
        for c in COLS:
            clamp_below(LAST, c)
        for c in COLS:
            clamp_above(LAST, c)

        fetch_half(far_late, b_gain, l_n5, [1], 1)
        fetch_half(sig_late, b_sig, l_n4, [0, 1], 1)
        fetch_half(near[1], b_gain, l_n3, [2, 3], 1)
        fetch_half(far_late, b_gain, l_n5, [2, 3], 1)
        fetch_half(sig_late, b_sig, l_n4, [2, 3], 1)
        z_dealt = dealt_tile("z_dealt")
        deal(nc.vector.tensor_copy, z_dealt, 0, z_planes[:])
        z_q = quantize_dealt("z_q", z_dealt)
        s_ps = [scores(z2_first, 0)]
        fused_step(0, 1)
        late_step(slice(1, 2))
        late_move(slice(0, 2))
        late_step(slice(2, PACK))
        late_move(slice(2, PACK))
        for t in range(PACK):
            open_scores(t, 0)
        s_ps.append(scores(quantize_z2(1), 1))

        open_scores(0, 1)
        nc.vector.tensor_scalar(s_val[1][:, COLS[1]], s_ps[1][1][:], SCORE_SCALE, None, ALU.mult)
        open_score_sig(1, 1)
        gate(0, HALVES)
        open_scores(2, 1)
        gate(1)
        open_scores(3, 1)
        fetch_st(0)
        gate(2)
        fetch_st(1)
        gate(3)
        finish(0)
        fetch_st(2)
        finish(1)
        fetch_st(LAST, SHRINKING)
        finish(2)
        finish(LAST, SHRINKING)
